import numpy as np
import ml_dtypes


def mxq(x, axis, fmt="e4m3"):
    dtype, down = {"e4m3": (ml_dtypes.float8_e4m3fn, 7), "e5m2": (ml_dtypes.float8_e5m2, 14)}[fmt]
    v = np.moveaxis(np.asarray(x, np.float32).astype(ml_dtypes.bfloat16).astype(np.float64), axis, -1)
    blocks = v.reshape(v.shape[:-1] + (-1, 32))
    amax = np.abs(blocks).max(-1, keepdims=True)
    byte = np.maximum(np.where(amax > 0, np.frexp(amax)[1] - 1 + 127, 0) - down, 1)
    scale = np.exp2(byte - 127.0)
    codes = (blocks / scale).astype(np.float32).astype(dtype).astype(np.float64)
    return np.moveaxis((codes * scale).reshape(v.shape), -1, axis)


WIDE = False


def mx_kscale(k):
    if not WIDE:
        return np.ones(k)
    levels = np.array([10, -10, 5, -5, 0])
    if k % 512:
        return np.exp2(np.random.permutation(np.resize(levels, k // 32))).repeat(32)
    a = np.empty((k // 512, 16))
    for p in range(k // 512):
        a[p, :8] = np.random.permutation(np.resize(levels, 8))
        for g in range(8):
            far = levels[np.abs(levels - a[p, g]) >= 10]
            a[p, g + 8] = far[np.random.randint(len(far))]
    return np.exp2(a.ravel()).repeat(32)


def f64(x):
    return np.asarray(x).astype(np.float64)


def striped(idx):
    return np.tile(idx.reshape(-1, 16).T, (8, 1)).astype(np.uint16)


def unstriped(offs):
    return offs[:16].T.reshape(-1).astype(np.int64)


E2M1 = np.array([0.0, 0.5, 1.0, 1.5, 2.0, 3.0, 4.0, 6.0, -0.0, -0.5, -1.0, -1.5, -2.0, -3.0, -4.0, -6.0])


def pack_weight(w, fmt):
    k, n = w.shape
    w = f64(np.asarray(w, np.float32).astype(ml_dtypes.bfloat16)).reshape(k // 32, 32, n)
    amax = np.abs(w).max(1)
    if fmt == "e4m3":
        byte = np.frexp(amax)[1] - 1 + 127 - 7
    else:
        mant, ex = np.frexp(amax / 6.0)
        byte = np.where(mant > 0.5, ex, ex - 1) + 127
    byte = np.clip(np.where(amax > 0, byte, 1), 1, 254)
    scaled = (w * np.exp2(127.0 - byte)[:, None, :]).reshape(k, n).astype(np.float32)
    by_word = np.ascontiguousarray(scaled.reshape(k // 512, 128, 4, n).transpose(0, 1, 3, 2))
    if fmt == "e4m3":
        words = by_word.astype(ml_dtypes.float8_e4m3fn).view(np.uint8)
    else:
        c = by_word.astype(ml_dtypes.float4_e2m1fn).view(np.uint8) & 0xF
        words = (c[..., 0::2] | (c[..., 1::2] << 4)).reshape(k // 512, 128, 2 * n)
    return np.ascontiguousarray(words), np.ascontiguousarray(byte.astype(np.uint8).reshape(k // 512, 16, n))


def unpack_weight(words, scales, fmt):
    g, _, n = scales.shape
    words = np.ascontiguousarray(words).reshape(g, 128, n, -1)
    if fmt == "e4m3":
        vals = words.view(ml_dtypes.float8_e4m3fn).astype(np.float64)
    else:
        nib = np.empty((g, 128, n, 4), np.uint8)
        nib[..., 0::2] = words & 0xF
        nib[..., 1::2] = words >> 4
        vals = E2M1[nib]
    vals = vals * np.repeat(np.exp2(scales.astype(np.float64) - 127.0), 8, axis=1)[..., None]
    return vals.transpose(0, 1, 3, 2).reshape(g * 512, n)


def gelu(v):
    return 0.5 * v * (1.0 + np.tanh(np.sqrt(2.0 / np.pi) * (v + 0.044715 * v**3)))


def bf(x):
    return np.asarray(x, np.float32).astype(ml_dtypes.bfloat16)


def planes(Y):
    n, m = Y.shape
    b = f64(bf(Y)).reshape(n // 32, 32, m)
    amax = np.abs(b).max(1)
    byte = np.clip(np.where(amax > 0, np.frexp(amax)[1] - 1 + 127 - 7, 1), 1, 254)
    codes = (b * np.exp2(127.0 - byte)[:, None, :]).reshape(n, m).astype(np.float32).astype(ml_dtypes.float8_e4m3fn).view(np.uint8)
    words = codes.reshape(n // 512, 128, 4, m).transpose(0, 1, 3, 2)
    return np.ascontiguousarray(words), np.ascontiguousarray(byte.astype(np.uint8).reshape(n // 512, 16, m))


K, T, S, P, H, N = 1536, 4096, 1024, 512, 512, 1024

def setup_inputs():
    n = np.random.standard_normal
    s = mx_kscale(K)[:, None]
    u = mx_kscale(H)[:, None]
    size = np.exp(0.8 * n(N))
    d = {}
    d["tab_words"], d["tab_scales"] = pack_weight(n((K, T)) * s, "e4m3")
    d["offs"] = striped(np.random.permutation(T)[:S])
    d["pos1"] = striped(np.random.permutation(S)[:P])
    d["pos2"] = striped(np.random.permutation(S)[:P])
    d["w1"] = (1.5 * n((K, H)) / K ** 0.5 / s).astype(np.float32)
    d["w2_words"], d["w2_scales"] = pack_weight(1.5 * n((K, H)) / K ** 0.5 / s, "e2m1")
    d["gain"] = (np.exp(0.3 * n(H)) * u[:, 0]).astype(np.float32)
    d["w3"] = (n((H, N)) / H ** 0.5 / u * size[None, :]).astype(np.float32)
    d["base"] = (n((N, S)) * size[:, None]).astype(np.float32)
    d["lam"] = np.random.uniform(0.4, 1.2, N).astype(np.float32)
    return d

def reference(tab_words, tab_scales, offs, pos1, pos2, w1, w2_words, w2_scales, gain, w3, base, lam):
    v = unpack_weight(tab_words, tab_scales, "e4m3")[:, unstriped(offs)]
    w2 = unpack_weight(w2_words, w2_scales, "e2m1")
    a = mxq(f64(w1), 0, "e4m3").T @ v
    b = w2.T @ v
    ga = 0.5 * a * (1.0 + np.tanh(0.7978845608028654 * (a + 0.044715 * a ** 3)))
    sb = b / (1.0 + np.exp(-b))
    h = f64(gain)[:, None] * (ga - sb)
    e = mxq(f64(w3), 0, "e4m3").T @ mxq(h, 0, "e4m3")
    g2 = np.maximum(e, f64(base))
    y = g2[:, unstriped(pos1)] - f64(lam)[:, None] * g2[:, unstriped(pos2)]
    words, scales = planes(y)
    return y, words, scales

@@ -1,0 +1,270 @@
+from contextlib import ExitStack
+
+import concourse.mybir as mybir
+
+K, T, S, PAIRS, H, N = 1536, 4096, 1024, 512, 512, 1024
+FLOPS = 2 * (2 * K * H * S + H * N * S)
+
+F32 = mybir.dt.float32
+BF16 = mybir.dt.bfloat16
+I32 = mybir.dt.int32
+U32 = mybir.dt.uint32
+U16 = mybir.dt.uint16
+U8 = mybir.dt.uint8
+FP8X4 = mybir.dt.float8_e4m3fn_x4
+FP4X4 = mybir.dt.float4_e2m1fn_x4
+ALU = mybir.AluOpType
+ACT = mybir.ActivationFunctionType
+
+P = 128
+PACK = 4
+K_PASS = P * PACK
+PASSES = K // K_PASS
+BANK = 512
+HALVES = S // BANK
+GROUPS = N // K_PASS
+QUADS = 4
+LIVE = 100
+
+
+def tile_list_vat_crosscheck_features_kernel(
+    tc, tab_words, tab_scales, offs, pos1, pos2, w1, w2_words, w2_scales, gain, w3, base, lam, out_0, out_1, out_2
+):
+    nc = tc.nc
+    with ExitStack() as ctx:
+        keep = ctx.enter_context(tc.tile_pool(name="keep", bufs=1))
+        quad = ctx.enter_context(tc.tile_pool(name="quad", bufs=3))
+        woven = ctx.enter_context(tc.tile_pool(name="woven", bufs=4))
+        gelus = ctx.enter_context(tc.tile_pool(name="gelus", bufs=5))
+        picks = ctx.enter_context(tc.tile_pool(name="picks", bufs=3))
+        psum = ctx.enter_context(tc.psum_pool(name="psum", bufs=1))
+
+        def bank(i):
+            return psum.tile([P, BANK], F32, name="bank%d" % i, tag="bank%d" % i)
+
+        idx = keep.tile([P, S // 16], U16, name="idx")
+        nc.sync.dma_start(idx[:], offs)
+
+        tab_planes = keep.tile([P, T // 4], I32, name="tab_planes", align_bytes=64)
+        w2_planes_raw = keep.tile([P, PASSES, H // 4], I32, name="w2_planes_raw", align_bytes=64)
+        moved_planes = keep.tile([P, PASSES - 1, S // 4], I32, name="moved_planes", align_bytes=64)
+        nc.vector.memset(tab_planes[:], 0)
+        nc.vector.memset(w2_planes_raw[:], 0)
+        nc.vector.memset(moved_planes[:], 0)
+
+        table = [keep.tile([P, T], I32, name="table%d" % a, align_bytes=64) for a in range(PASSES)]
+
+        def load_table(a):
+            nc.sync.dma_start(table[a][:], tab_words[a].rearrange("p t i -> p (t i)").bitcast(I32))
+
+        load_table(0)
+        for q in range(QUADS):
+            nc.gpsimd.dma_start(
+                tab_planes[32 * q : 32 * q + 4 * PASSES, :], tab_scales[:, 4 * q : 4 * q + 4, :].bitcast(I32)
+            )
+        w2_raw = keep.tile([P, PASSES, 2 * H // 4], I32, name="w2_raw", align_bytes=64)
+        nc.scalar.dma_start(w2_raw[:], w2_words.bitcast(I32).rearrange("a p c -> p a c"))
+        load_table(1)
+        for q in range(QUADS):
+            nc.gpsimd.dma_start(
+                w2_planes_raw[32 * q : 32 * q + 4, :, :],
+                w2_scales[:, 4 * q : 4 * q + 4, :].bitcast(I32).rearrange("a r c -> r a c"),
+            )
+        load_table(2)
+        gain_sb = keep.tile([P, PACK], F32, name="gain_sb")
+        nc.scalar.dma_start(gain_sb[:], gain.rearrange("(p t) -> p t", t=PACK))
+
+        w1_raw = []
+        for a in range(PASSES):
+            raw = quad.tile([P, PACK, H], F32, name="w1_raw%d" % a, tag="quad")
+            nc.sync.dma_start(raw[:], w1[a * K_PASS : (a + 1) * K_PASS, :].rearrange("(p i) c -> p i c", i=PACK))
+            w1_raw.append(raw)
+
+        v_planes = keep.tile([P, S], U8, name="v_planes", align_bytes=64)
+        nc.vector.tensor_copy(v_planes[:], tab_planes[:].bitcast(U8).indirect(idx[:]))
+        for a in range(1, PASSES):
+            nc.gpsimd.dma_start(moved_planes[0:LIVE, a - 1, :], v_planes[4 * a : 4 * a + LIVE, :].bitcast(I32))
+
+        def v_scale(a, half):
+            cols = slice(half * BANK, (half + 1) * BANK)
+            if a == 0:
+                return v_planes[:, cols]
+            return moved_planes[:, a - 1, :].bitcast(U8)[:, cols]
+
+        w2_codes = [keep.tile([P, 2 * H], U8, name="w2_codes%d" % a, align_bytes=64) for a in range(PASSES)]
+        for a in range(PASSES):
+            nc.vector.tensor_copy(
+                w2_codes[a][:].rearrange("p (t m b) -> p m t b", t=PACK, b=2),
+                w2_raw[:, a, :].bitcast(U8).rearrange("p (m t b) -> p m t b", t=PACK, b=2),
+            )
+        w2_planes = keep.tile([P, PASSES, H], U8, name="w2_planes", align_bytes=64)
+        nc.vector.tensor_copy(
+            w2_planes[:].rearrange("p a (t m) -> p a m t", t=PACK),
+            w2_planes_raw[:].bitcast(U8).rearrange("p a (m t) -> p a m t", t=PACK),
+        )
+
+        v_words = {}
+        b_acc = {(half, t): bank(PACK * half + t) for half in range(HALVES) for t in range(PACK)}
+        for a in range(PASSES):
+            for half in range(HALVES):
+                words = keep.tile([P, BANK], U32, name="v_words%d_%d" % (a, half), align_bytes=64)
+                cols = slice(half * BANK // 16, (half + 1) * BANK // 16)
+                nc.vector.tensor_copy(words[:], table[a][:].bitcast(U32).indirect(idx[:, cols]))
+                v_words[a, half] = words
+                for t in range(PACK):
+                    nc.tensor.matmul_mx(
+                        out=b_acc[half, t][:],
+                        lhsT=w2_codes[a][:, 2 * P * t : 2 * P * (t + 1)].bitcast(FP4X4),
+                        lhsT_scale=w2_planes[:, a, P * t : P * (t + 1)],
+                        rhs=words[:].bitcast(FP8X4),
+                        rhs_scale=v_scale(a, half),
+                        start=(a == 0),
+                        stop=(a == PASSES - 1),
+                    )
+
+        gained_silu = {}
+        for half in range(HALVES):
+            for t in range(PACK):
+                sb = keep.tile([P, BANK], F32, name="silu%d_%d" % (half, t))
+                nc.scalar.activation(sb[:], b_acc[half, t][:], ACT.Silu)
+                gained_silu[half, t] = sb
+
+        def quantize_weight(raw, name, cast, t_runs):
+            codes = keep.tile([P, K_PASS], U32, name=name + "_codes", align_bytes=64)
+            planes = keep.tile([P, K_PASS], U8, name=name + "_planes", align_bytes=64)
+            dealt = woven.tile([P, PACK * K_PASS], BF16, name=name + "_dealt", tag="woven", align_bytes=64)
+            for t0, t1 in t_runs:
+                cast(
+                    dealt[:, K_PASS * t0 : K_PASS * t1].rearrange("p (t m i) -> p m i t", m=P, i=PACK),
+                    raw[:].rearrange("p i (m t) -> p m i t", t=PACK)[:, :, :, t0:t1],
+                )
+                nc.vector.quantize_mx(
+                    out=codes[:, P * t0 : P * t1].bitcast(FP8X4),
+                    scales=planes[:, P * t0 : P * t1],
+                    in_=dealt[:, K_PASS * t0 : K_PASS * t1],
+                )
+            return codes, planes
+
+        a_acc = {(half, t): bank(PACK * half + t) for half in range(HALVES) for t in range(PACK)}
+        for a in range(PASSES):
+            last = a == PASSES - 1
+            codes, planes = quantize_weight(
+                w1_raw[a], "w1q%d" % a, nc.vector.tensor_copy, [(0, 2), (2, 4)] if last else [(0, 4)]
+            )
+            if not last:
+                for t in range(PACK):
+                    sb = gained_silu[a, t]
+                    nc.vector.tensor_scalar(sb[:], sb[:], gain_sb[:, t : t + 1], None, ALU.mult)
+            for half in range(HALVES):
+                for t in range(PACK):
+                    nc.tensor.matmul_mx(
+                        out=a_acc[half, t][:],
+                        lhsT=codes[:, P * t : P * (t + 1)].bitcast(FP8X4),
+                        lhsT_scale=planes[:, P * t : P * (t + 1)],
+                        rhs=v_words[a, half][:].bitcast(FP8X4),
+                        rhs_scale=v_scale(a, half),
+                        start=(a == 0),
+                        stop=last,
+                    )
+
+        w3_raw, g2 = [], []
+        first = keep.tile([P, PAIRS // 16], U16, name="first")
+        second = keep.tile([P, PAIRS // 16], U16, name="second")
+        lam_sb = keep.tile([P, GROUPS, PACK], F32, name="lam_sb")
+        base_rows = base.rearrange("(g p t) j -> g t p j", p=P, t=PACK)
+        for g in range(GROUPS):
+            raw = keep.tile([P, PACK, K_PASS], F32, name="w3_raw%d" % g)
+            nc.sync.dma_start(raw[:], w3[:, g * K_PASS : (g + 1) * K_PASS].rearrange("(p i) c -> p i c", i=PACK))
+            w3_raw.append(raw)
+            if g == 0:
+                nc.sync.dma_start(first[:], pos1)
+                nc.sync.dma_start(second[:], pos2)
+                nc.sync.dma_start(lam_sb[:], lam.rearrange("(g p t) -> p g t", p=P, t=PACK))
+            for t in range(PACK):
+                rows = keep.tile([P, S], F32, name="g2_%d_%d" % (g, t))
+                nc.sync.dma_start(rows[:], base_rows[g, t])
+                g2.append(rows)
+
+        h_q = []
+        for half in range(HALVES):
+            h_rows = keep.tile([P, PACK, BANK], BF16, name="h_rows%d" % half)
+            for t in range(PACK):
+                ga = gelus.tile([P, BANK], F32, name="gelu%d_%d" % (half, t), tag="gelu")
+                nc.scalar.activation(ga[:], a_acc[half, t][:], ACT.Gelu_apprx_tanh)
+                nc.vector.scalar_tensor_tensor(
+                    h_rows[:, t, :], ga[:], gain_sb[:, t : t + 1], gained_silu[half, t][:], ALU.mult, ALU.subtract
+                )
+            h_woven = woven.tile([P, BANK * PACK], BF16, name="h_woven%d" % half, tag="woven", align_bytes=64)
+            weave = nc.vector.tensor_copy if half == 0 else nc.scalar.copy
+            weave(
+                h_woven[:].rearrange("p (c i t) -> p c t i", i=4, t=PACK),
+                h_rows[:].rearrange("p t (c i) -> p c t i", i=4),
+            )
+            codes = keep.tile([P, BANK], U32, name="h_codes%d" % half, align_bytes=64)
+            planes = keep.tile([P, BANK], U8, name="h_planes%d" % half, align_bytes=64)
+            nc.vector.quantize_mx(out=codes[:].bitcast(FP8X4), scales=planes[:], in_=h_woven[:])
+            h_q.append((codes, planes))
+            if half == 0:
+                w3_q = [quantize_weight(w3_raw[0], "w3q0", nc.scalar.copy, [(0, 2), (2, 4)])]
+        w3_q.append(quantize_weight(w3_raw[1], "w3q1", nc.scalar.copy, [(0, 4)]))
+
+        def second_stage(s, half):
+            g, t = divmod(s, PACK)
+            acc = bank(PACK * half + t)
+            codes, planes = w3_q[g]
+            nc.tensor.matmul_mx(
+                out=acc[:],
+                lhsT=codes[:, P * t : P * (t + 1)].bitcast(FP8X4),
+                lhsT_scale=planes[:, P * t : P * (t + 1)],
+                rhs=h_q[half][0][:].bitcast(FP8X4),
+                rhs_scale=h_q[half][1][:],
+                start=True,
+                stop=True,
+            )
+            cols = slice(half * BANK, (half + 1) * BANK)
+            nc.vector.tensor_tensor(g2[s][:, cols], acc[:], g2[s][:, cols], ALU.max)
+
+        out_rows = out_0.rearrange("(g p t) m -> g t p m", p=P, t=PACK)
+        y = [quad.tile([P, PACK, PAIRS], F32, name="y%d" % g, tag="quad") for g in range(GROUPS)]
+        buyers = {}
+
+        def pick_buyer(s):
+            g, t = divmod(s, PACK)
+            u = picks.tile([P, PAIRS], F32, name="buyer%d" % s, tag="buyer")
+            nc.vector.tensor_copy(u[:], g2[s][:].indirect(second[:]))
+            nc.scalar.activation(u[:], u[:], ACT.Copy, scale=lam_sb[:, g, t : t + 1])
+            buyers[s] = u
+
+        def pick_seller(s):
+            g, t = divmod(s, PACK)
+            nc.vector.tensor_tensor(y[g][:, t, :], g2[s][:].indirect(first[:]), buyers[s][:], ALU.subtract)
+            nc.sync.dma_start(out_rows[g, t], y[g][:, t, :])
+
+        def planes_of(g):
+            y_woven = woven.tile([P, PAIRS * PACK], BF16, name="y_woven%d" % g, tag="woven", align_bytes=64)
+            nc.scalar.copy(
+                y_woven[:].rearrange("p (c i t) -> p c t i", i=4, t=PACK),
+                y[g][:].rearrange("p t (c i) -> p c t i", i=4),
+            )
+            codes = keep.tile([P, PAIRS], U32, name="y_codes%d" % g, align_bytes=64)
+            planes = keep.tile([P, PAIRS], U8, name="y_planes%d" % g, align_bytes=64)
+            nc.vector.quantize_mx(out=codes[:].bitcast(FP8X4), scales=planes[:], in_=y_woven[:])
+            nc.sync.dma_start(out_1[g].rearrange("p m t -> p (m t)").bitcast(I32), codes[:].bitcast(I32))
+            for q in range(QUADS):
+                nc.sync.dma_start(
+                    out_2[g, 4 * q : 4 * q + 4, :].bitcast(I32), planes[32 * q : 32 * q + 4, :].bitcast(I32)
+                )
+
+        slices = GROUPS * PACK
+        for s in range(PACK):
+            second_stage(s, 0)
+        for s in range(slices + 1):
+            if s < slices:
+                if s >= PACK:
+                    second_stage(s, 0)
+                second_stage(s, 1)
+                pick_buyer(s)
+            if s > 0:
+                pick_seller(s - 1)
+                if s % PACK == 0:
+                    planes_of(s // PACK - 1)

@@ -25,6 +25,7 @@ HALVES = S // BANK
 GROUPS = N // K_PASS
 QUADS = 4
 LIVE = 100
+KIB = 1024
 
 
 def tile_list_vat_crosscheck_features_kernel(
@@ -33,7 +34,7 @@ def tile_list_vat_crosscheck_features_kernel(
     nc = tc.nc
     with ExitStack() as ctx:
         keep = ctx.enter_context(tc.tile_pool(name="keep", bufs=1))
-        quad = ctx.enter_context(tc.tile_pool(name="quad", bufs=3))
+        shared = ctx.enter_context(tc.tile_pool(name="shared", bufs=1))
         woven = ctx.enter_context(tc.tile_pool(name="woven", bufs=4))
         gelus = ctx.enter_context(tc.tile_pool(name="gelus", bufs=5))
         picks = ctx.enter_context(tc.tile_pool(name="picks", bufs=3))
@@ -44,52 +45,35 @@ def tile_list_vat_crosscheck_features_kernel(
 
         idx = keep.tile([P, S // 16], U16, name="idx")
         nc.sync.dma_start(idx[:], offs)
+        w2_raw = shared.tile([P, PASSES, 2 * H // 4], I32, name="w2_raw", offset=36 * KIB - 1536)
+        nc.sync.dma_start(w2_raw[:], w2_words.bitcast(I32).rearrange("a p c -> p a c"))
+        first = keep.tile([P, PAIRS // 16], U16, name="first")
+        second = keep.tile([P, PAIRS // 16], U16, name="second")
 
-        tab_planes = keep.tile([P, T // 4], I32, name="tab_planes", align_bytes=64)
-        w2_planes_raw = keep.tile([P, PASSES, H // 4], I32, name="w2_planes_raw", align_bytes=64)
+        tab_planes = shared.tile([P, T // 4], I32, name="tab_planes", offset=0)
+        w2_planes_raw = shared.tile([P, PASSES, H // 4], I32, name="w2_planes_raw", offset=52 * KIB)
         moved_planes = keep.tile([P, PASSES - 1, S // 4], I32, name="moved_planes", align_bytes=64)
         nc.vector.memset(tab_planes[:], 0)
         nc.vector.memset(w2_planes_raw[:], 0)
         nc.vector.memset(moved_planes[:], 0)
 
-        table = [keep.tile([P, T], I32, name="table%d" % a, align_bytes=64) for a in range(PASSES)]
+        table = [shared.tile([P, T], I32, name="table%d" % a, offset=(4 + 16 * a) * KIB) for a in range(PASSES)]
 
         def load_table(a):
             nc.sync.dma_start(table[a][:], tab_words[a].rearrange("p t i -> p (t i)").bitcast(I32))
 
+        nc.sync.dma_start(first[:], pos1)
+        nc.sync.dma_start(second[:], pos2)
         load_table(0)
         for q in range(QUADS):
-            nc.gpsimd.dma_start(
+            nc.scalar.dma_start(
                 tab_planes[32 * q : 32 * q + 4 * PASSES, :], tab_scales[:, 4 * q : 4 * q + 4, :].bitcast(I32)
             )
-        w2_raw = keep.tile([P, PASSES, 2 * H // 4], I32, name="w2_raw", align_bytes=64)
-        nc.scalar.dma_start(w2_raw[:], w2_words.bitcast(I32).rearrange("a p c -> p a c"))
-        load_table(1)
         for q in range(QUADS):
-            nc.gpsimd.dma_start(
+            nc.scalar.dma_start(
                 w2_planes_raw[32 * q : 32 * q + 4, :, :],
                 w2_scales[:, 4 * q : 4 * q + 4, :].bitcast(I32).rearrange("a r c -> r a c"),
             )
-        load_table(2)
-        gain_sb = keep.tile([P, PACK], F32, name="gain_sb")
-        nc.scalar.dma_start(gain_sb[:], gain.rearrange("(p t) -> p t", t=PACK))
-
-        w1_raw = []
-        for a in range(PASSES):
-            raw = quad.tile([P, PACK, H], F32, name="w1_raw%d" % a, tag="quad")
-            nc.sync.dma_start(raw[:], w1[a * K_PASS : (a + 1) * K_PASS, :].rearrange("(p i) c -> p i c", i=PACK))
-            w1_raw.append(raw)
-
-        v_planes = keep.tile([P, S], U8, name="v_planes", align_bytes=64)
-        nc.vector.tensor_copy(v_planes[:], tab_planes[:].bitcast(U8).indirect(idx[:]))
-        for a in range(1, PASSES):
-            nc.gpsimd.dma_start(moved_planes[0:LIVE, a - 1, :], v_planes[4 * a : 4 * a + LIVE, :].bitcast(I32))
-
-        def v_scale(a, half):
-            cols = slice(half * BANK, (half + 1) * BANK)
-            if a == 0:
-                return v_planes[:, cols]
-            return moved_planes[:, a - 1, :].bitcast(U8)[:, cols]
 
         w2_codes = [keep.tile([P, 2 * H], U8, name="w2_codes%d" % a, align_bytes=64) for a in range(PASSES)]
         for a in range(PASSES):
@@ -97,11 +81,30 @@ def tile_list_vat_crosscheck_features_kernel(
                 w2_codes[a][:].rearrange("p (t m b) -> p m t b", t=PACK, b=2),
                 w2_raw[:, a, :].bitcast(U8).rearrange("p (m t b) -> p m t b", t=PACK, b=2),
             )
+        load_table(1)
+        load_table(2)
+
+        v_planes = keep.tile([P, S], U8, name="v_planes", align_bytes=64)
+        nc.vector.tensor_copy(v_planes[:], tab_planes[:].bitcast(U8).indirect(idx[:]))
+        for a in range(1, PASSES):
+            nc.scalar.dma_start(moved_planes[0:LIVE, a - 1, :], v_planes[4 * a : 4 * a + LIVE, :].bitcast(I32))
+
+        def v_scale(a, half):
+            cols = slice(half * BANK, (half + 1) * BANK)
+            if a == 0:
+                return v_planes[:, cols]
+            return moved_planes[:, a - 1, :].bitcast(U8)[:, cols]
+
         w2_planes = keep.tile([P, PASSES, H], U8, name="w2_planes", align_bytes=64)
         nc.vector.tensor_copy(
             w2_planes[:].rearrange("p a (t m) -> p a m t", t=PACK),
             w2_planes_raw[:].bitcast(U8).rearrange("p a (m t) -> p a m t", t=PACK),
         )
+
+        gain_sb = shared.tile([P, PACK], F32, name="gain_sb", offset=52 * KIB)
+        nc.scalar.dma_start(gain_sb[:], gain.rearrange("(p t) -> p t", t=PACK))
+        lam_sb = shared.tile([P, GROUPS, PACK], F32, name="lam_sb", offset=52 * KIB + 64)
+        nc.scalar.dma_start(lam_sb[:], lam.rearrange("(g p t) -> p g t", p=P, t=PACK))
 
         v_words = {}
         b_acc = {(half, t): bank(PACK * half + t) for half in range(HALVES) for t in range(PACK)}
@@ -122,17 +125,23 @@ def tile_list_vat_crosscheck_features_kernel(
                         stop=(a == PASSES - 1),
                     )
 
-        gained_silu = {}
+        w1_raw = []
+        for a, place in enumerate((0, 20, 28)):
+            raw = shared.tile([P, PACK, H], F32, name="w1_raw%d" % a, offset=place * KIB)
+            nc.sync.dma_start(raw[:], w1[a * K_PASS : (a + 1) * K_PASS, :].rearrange("(p i) c -> p i c", i=PACK))
+            w1_raw.append(raw)
+
+        silu, gained_silu = {}, {}
         for half in range(HALVES):
             for t in range(PACK):
-                sb = keep.tile([P, BANK], F32, name="silu%d_%d" % (half, t))
-                nc.scalar.activation(sb[:], b_acc[half, t][:], ACT.Silu)
-                gained_silu[half, t] = sb
+                place = 54 + 2 * (PACK * half + t)
+                silu[half, t] = shared.tile([P, BANK], F32, name="silu%d_%d" % (half, t), offset=place * KIB)
+                nc.scalar.activation(silu[half, t][:], b_acc[half, t][:], ACT.Silu)
 
-        def quantize_weight(raw, name, cast, t_runs):
+        def quantize_weight(raw, name, cast, t_runs, place):
             codes = keep.tile([P, K_PASS], U32, name=name + "_codes", align_bytes=64)
             planes = keep.tile([P, K_PASS], U8, name=name + "_planes", align_bytes=64)
-            dealt = woven.tile([P, PACK * K_PASS], BF16, name=name + "_dealt", tag="woven", align_bytes=64)
+            dealt = shared.tile([P, PACK * K_PASS], BF16, name=name + "_dealt", offset=place * KIB, align_bytes=64)
             for t0, t1 in t_runs:
                 cast(
                     dealt[:, K_PASS * t0 : K_PASS * t1].rearrange("p (t m i) -> p m i t", m=P, i=PACK),
@@ -149,12 +158,14 @@ def tile_list_vat_crosscheck_features_kernel(
         for a in range(PASSES):
             last = a == PASSES - 1
             codes, planes = quantize_weight(
-                w1_raw[a], "w1q%d" % a, nc.vector.tensor_copy, [(0, 2), (2, 4)] if last else [(0, 4)]
+                w1_raw[a], "w1q%d" % a, nc.vector.tensor_copy, [(0, 2), (2, 4)] if last else [(0, 4)], (36, 90, 66)[a]
             )
             if not last:
                 for t in range(PACK):
-                    sb = gained_silu[a, t]
-                    nc.vector.tensor_scalar(sb[:], sb[:], gain_sb[:, t : t + 1], None, ALU.mult)
+                    place = 70 + 2 * (PACK * a + t)
+                    sb = shared.tile([P, BANK], F32, name="gained%d_%d" % (a, t), offset=place * KIB)
+                    nc.vector.tensor_scalar(sb[:], silu[a, t][:], gain_sb[:, t : t + 1], None, ALU.mult)
+                    gained_silu[a, t] = sb
             for half in range(HALVES):
                 for t in range(PACK):
                     nc.tensor.matmul_mx(
@@ -167,27 +178,26 @@ def tile_list_vat_crosscheck_features_kernel(
                         stop=last,
                     )
 
-        w3_raw, g2 = [], []
-        first = keep.tile([P, PAIRS // 16], U16, name="first")
-        second = keep.tile([P, PAIRS // 16], U16, name="second")
-        lam_sb = keep.tile([P, GROUPS, PACK], F32, name="lam_sb")
         base_rows = base.rearrange("(g p t) j -> g t p j", p=P, t=PACK)
-        for g in range(GROUPS):
-            raw = keep.tile([P, PACK, K_PASS], F32, name="w3_raw%d" % g)
+
+        def load_w3(g, place):
+            raw = shared.tile([P, PACK, K_PASS], F32, name="w3_raw%d" % g, offset=place * KIB)
             nc.sync.dma_start(raw[:], w3[:, g * K_PASS : (g + 1) * K_PASS].rearrange("(p i) c -> p i c", i=PACK))
-            w3_raw.append(raw)
-            if g == 0:
-                nc.sync.dma_start(first[:], pos1)
-                nc.sync.dma_start(second[:], pos2)
-                nc.sync.dma_start(lam_sb[:], lam.rearrange("(g p t) -> p g t", p=P, t=PACK))
-            for t in range(PACK):
-                rows = keep.tile([P, S], F32, name="g2_%d_%d" % (g, t))
-                nc.sync.dma_start(rows[:], base_rows[g, t])
-                g2.append(rows)
+            return raw
+
+        def load_base(s, place):
+            rows = shared.tile([P, S], F32, name="g2_%d" % s, offset=place * KIB)
+            nc.sync.dma_start(rows[:], base_rows[s // PACK, s % PACK])
+            return rows
+
+        w3_raw = [load_w3(0, 40)]
+        g2 = [load_base(s, place) for s, place in enumerate((48, 0, 4, 36))]
+        w3_raw.append(load_w3(1, 20))
+        g2.extend([load_base(4, 28), load_base(5, 32)])
 
         h_q = []
         for half in range(HALVES):
-            h_rows = keep.tile([P, PACK, BANK], BF16, name="h_rows%d" % half)
+            h_rows = shared.tile([P, PACK, BANK], BF16, name="h_rows%d" % half, offset=(94 - 8 * half) * KIB)
             for t in range(PACK):
                 ga = gelus.tile([P, BANK], F32, name="gelu%d_%d" % (half, t), tag="gelu")
                 nc.scalar.activation(ga[:], a_acc[half, t][:], ACT.Gelu_apprx_tanh)
@@ -205,8 +215,9 @@ def tile_list_vat_crosscheck_features_kernel(
             nc.vector.quantize_mx(out=codes[:].bitcast(FP8X4), scales=planes[:], in_=h_woven[:])
             h_q.append((codes, planes))
             if half == 0:
-                w3_q = [quantize_weight(w3_raw[0], "w3q0", nc.scalar.copy, [(0, 2), (2, 4)])]
-        w3_q.append(quantize_weight(w3_raw[1], "w3q1", nc.scalar.copy, [(0, 4)]))
+                w3_q = [quantize_weight(w3_raw[0], "w3q0", nc.scalar.copy, [(0, 2), (2, 4)], 74)]
+        g2.extend([load_base(6, 40), load_base(7, 44)])
+        w3_q.append(quantize_weight(w3_raw[1], "w3q1", nc.scalar.copy, [(0, 4)], 86))
 
         def second_stage(s, half):
             g, t = divmod(s, PACK)
@@ -225,7 +236,7 @@ def tile_list_vat_crosscheck_features_kernel(
             nc.vector.tensor_tensor(g2[s][:, cols], acc[:], g2[s][:, cols], ALU.max)
 
         out_rows = out_0.rearrange("(g p t) m -> g t p m", p=P, t=PACK)
-        y = [quad.tile([P, PACK, PAIRS], F32, name="y%d" % g, tag="quad") for g in range(GROUPS)]
+        y = [keep.tile([P, PACK, PAIRS], F32, name="y%d" % g) for g in range(GROUPS)]
         buyers = {}
 
         def pick_buyer(s):

@@ -45,19 +45,19 @@ def tile_list_vat_crosscheck_features_kernel(
 
         idx = keep.tile([P, S // 16], U16, name="idx")
         nc.sync.dma_start(idx[:], offs)
-        w2_raw = shared.tile([P, PASSES, 2 * H // 4], I32, name="w2_raw", offset=36 * KIB - 1536)
+        w2_raw = shared.tile([P, PASSES, 2 * H // 4], I32, name="w2_raw", offset=38 * KIB - 1536)
         nc.sync.dma_start(w2_raw[:], w2_words.bitcast(I32).rearrange("a p c -> p a c"))
         first = keep.tile([P, PAIRS // 16], U16, name="first")
         second = keep.tile([P, PAIRS // 16], U16, name="second")
 
-        tab_planes = shared.tile([P, T // 4], I32, name="tab_planes", offset=0)
-        w2_planes_raw = shared.tile([P, PASSES, H // 4], I32, name="w2_planes_raw", offset=52 * KIB)
+        tab_planes = shared.tile([P, T // 4], I32, name="tab_planes", offset=2 * KIB)
+        w2_planes_raw = shared.tile([P, PASSES, H // 4], I32, name="w2_planes_raw", offset=0)
         moved_planes = keep.tile([P, PASSES - 1, S // 4], I32, name="moved_planes", align_bytes=64)
         nc.vector.memset(tab_planes[:], 0)
         nc.vector.memset(w2_planes_raw[:], 0)
         nc.vector.memset(moved_planes[:], 0)
 
-        table = [shared.tile([P, T], I32, name="table%d" % a, offset=(4 + 16 * a) * KIB) for a in range(PASSES)]
+        table = [shared.tile([P, T], I32, name="table%d" % a, offset=(6 + 16 * a) * KIB) for a in range(PASSES)]
 
         def load_table(a):
             nc.sync.dma_start(table[a][:], tab_words[a].rearrange("p t i -> p (t i)").bitcast(I32))
@@ -70,7 +70,7 @@ def tile_list_vat_crosscheck_features_kernel(
                 tab_planes[32 * q : 32 * q + 4 * PASSES, :], tab_scales[:, 4 * q : 4 * q + 4, :].bitcast(I32)
             )
         for q in range(QUADS):
-            nc.scalar.dma_start(
+            nc.gpsimd.dma_start(
                 w2_planes_raw[32 * q : 32 * q + 4, :, :],
                 w2_scales[:, 4 * q : 4 * q + 4, :].bitcast(I32).rearrange("a r c -> r a c"),
             )
@@ -78,8 +78,8 @@ def tile_list_vat_crosscheck_features_kernel(
         w2_codes = [keep.tile([P, 2 * H], U8, name="w2_codes%d" % a, align_bytes=64) for a in range(PASSES)]
         for a in range(PASSES):
             nc.vector.tensor_copy(
-                w2_codes[a][:].rearrange("p (t m b) -> p m t b", t=PACK, b=2),
-                w2_raw[:, a, :].bitcast(U8).rearrange("p (m t b) -> p m t b", t=PACK, b=2),
+                w2_codes[a][:].rearrange("p (t c m b) -> p c t m b", t=PACK, m=8, b=2),
+                w2_raw[:, a, :].bitcast(U8).rearrange("p (c m t b) -> p c t m b", t=PACK, m=8, b=2),
             )
         load_table(1)
         load_table(2)
@@ -87,7 +87,7 @@ def tile_list_vat_crosscheck_features_kernel(
         v_planes = keep.tile([P, S], U8, name="v_planes", align_bytes=64)
         nc.vector.tensor_copy(v_planes[:], tab_planes[:].bitcast(U8).indirect(idx[:]))
         for a in range(1, PASSES):
-            nc.scalar.dma_start(moved_planes[0:LIVE, a - 1, :], v_planes[4 * a : 4 * a + LIVE, :].bitcast(I32))
+            nc.gpsimd.dma_start(moved_planes[0:LIVE, a - 1, :], v_planes[4 * a : 4 * a + LIVE, :].bitcast(I32))
 
         def v_scale(a, half):
             cols = slice(half * BANK, (half + 1) * BANK)
@@ -97,20 +97,21 @@ def tile_list_vat_crosscheck_features_kernel(
 
         w2_planes = keep.tile([P, PASSES, H], U8, name="w2_planes", align_bytes=64)
         nc.vector.tensor_copy(
-            w2_planes[:].rearrange("p a (t m) -> p a m t", t=PACK),
-            w2_planes_raw[:].bitcast(U8).rearrange("p a (m t) -> p a m t", t=PACK),
+            w2_planes[:].rearrange("p a (t c m) -> p a c t m", t=PACK, m=16),
+            w2_planes_raw[:].bitcast(U8).rearrange("p a (c m t) -> p a c t m", t=PACK, m=16),
         )
 
-        gain_sb = shared.tile([P, PACK], F32, name="gain_sb", offset=52 * KIB)
+        gain_sb = shared.tile([P, PACK], F32, name="gain_sb", offset=0)
         nc.scalar.dma_start(gain_sb[:], gain.rearrange("(p t) -> p t", t=PACK))
-        lam_sb = shared.tile([P, GROUPS, PACK], F32, name="lam_sb", offset=52 * KIB + 64)
+        lam_sb = shared.tile([P, GROUPS, PACK], F32, name="lam_sb", offset=64)
         nc.scalar.dma_start(lam_sb[:], lam.rearrange("(g p t) -> p g t", p=P, t=PACK))
 
         v_words = {}
         b_acc = {(half, t): bank(PACK * half + t) for half in range(HALVES) for t in range(PACK)}
         for a in range(PASSES):
             for half in range(HALVES):
-                words = keep.tile([P, BANK], U32, name="v_words%d_%d" % (a, half), align_bytes=64)
+                place = (1 + 2 * half) if a == 1 else (100 + 2 * a + 2 * half)
+                words = shared.tile([P, BANK], U32, name="v_words%d_%d" % (a, half), offset=place * KIB, align_bytes=64)
                 cols = slice(half * BANK // 16, (half + 1) * BANK // 16)
                 nc.vector.tensor_copy(words[:], table[a][:].bitcast(U32).indirect(idx[:, cols]))
                 v_words[a, half] = words
@@ -126,8 +127,8 @@ def tile_list_vat_crosscheck_features_kernel(
                     )
 
         w1_raw = []
-        for a, place in enumerate((0, 20, 28)):
-            raw = shared.tile([P, PACK, H], F32, name="w1_raw%d" % a, offset=place * KIB)
+        for a, place in enumerate((4, 20, 28)):
+            raw = shared.tile([P, PACK, H], F32, name="w1_raw%d" % a, offset=(2 + place) * KIB)
             nc.sync.dma_start(raw[:], w1[a * K_PASS : (a + 1) * K_PASS, :].rearrange("(p i) c -> p i c", i=PACK))
             w1_raw.append(raw)
 
@@ -135,17 +136,17 @@ def tile_list_vat_crosscheck_features_kernel(
         for half in range(HALVES):
             for t in range(PACK):
                 place = 54 + 2 * (PACK * half + t)
-                silu[half, t] = shared.tile([P, BANK], F32, name="silu%d_%d" % (half, t), offset=place * KIB)
+                silu[half, t] = shared.tile([P, BANK], F32, name="silu%d_%d" % (half, t), offset=(2 + place) * KIB)
                 nc.scalar.activation(silu[half, t][:], b_acc[half, t][:], ACT.Silu)
 
         def quantize_weight(raw, name, cast, t_runs, place):
             codes = keep.tile([P, K_PASS], U32, name=name + "_codes", align_bytes=64)
             planes = keep.tile([P, K_PASS], U8, name=name + "_planes", align_bytes=64)
-            dealt = shared.tile([P, PACK * K_PASS], BF16, name=name + "_dealt", offset=place * KIB, align_bytes=64)
+            dealt = shared.tile([P, PACK * K_PASS], BF16, name=name + "_dealt", offset=(2 + place) * KIB, align_bytes=64)
             for t0, t1 in t_runs:
                 cast(
-                    dealt[:, K_PASS * t0 : K_PASS * t1].rearrange("p (t m i) -> p m i t", m=P, i=PACK),
-                    raw[:].rearrange("p i (m t) -> p m i t", t=PACK)[:, :, :, t0:t1],
+                    dealt[:, K_PASS * t0 : K_PASS * t1].rearrange("p (u e m i) -> p u m e i", e=2, m=P, i=PACK),
+                    raw[:].rearrange("p i (m u e) -> p u m e i", u=2, e=2)[:, t0 // 2 : t1 // 2],
                 )
                 nc.vector.quantize_mx(
                     out=codes[:, P * t0 : P * t1].bitcast(FP8X4),
@@ -163,7 +164,7 @@ def tile_list_vat_crosscheck_features_kernel(
             if not last:
                 for t in range(PACK):
                     place = 70 + 2 * (PACK * a + t)
-                    sb = shared.tile([P, BANK], F32, name="gained%d_%d" % (a, t), offset=place * KIB)
+                    sb = shared.tile([P, BANK], F32, name="gained%d_%d" % (a, t), offset=(2 + place) * KIB)
                     nc.vector.tensor_scalar(sb[:], silu[a, t][:], gain_sb[:, t : t + 1], None, ALU.mult)
                     gained_silu[a, t] = sb
             for half in range(HALVES):
@@ -181,23 +182,23 @@ def tile_list_vat_crosscheck_features_kernel(
         base_rows = base.rearrange("(g p t) j -> g t p j", p=P, t=PACK)
 
         def load_w3(g, place):
-            raw = shared.tile([P, PACK, K_PASS], F32, name="w3_raw%d" % g, offset=place * KIB)
+            raw = shared.tile([P, PACK, K_PASS], F32, name="w3_raw%d" % g, offset=(2 + place) * KIB)
             nc.sync.dma_start(raw[:], w3[:, g * K_PASS : (g + 1) * K_PASS].rearrange("(p i) c -> p i c", i=PACK))
             return raw
 
         def load_base(s, place):
-            rows = shared.tile([P, S], F32, name="g2_%d" % s, offset=place * KIB)
+            rows = shared.tile([P, S], F32, name="g2_%d" % s, offset=(2 + place) * KIB)
             nc.sync.dma_start(rows[:], base_rows[s // PACK, s % PACK])
             return rows
 
         w3_raw = [load_w3(0, 40)]
-        g2 = [load_base(s, place) for s, place in enumerate((48, 0, 4, 36))]
+        g2 = [load_base(s, place) for s, place in enumerate((48, 4, 8, 36))]
         w3_raw.append(load_w3(1, 20))
         g2.extend([load_base(4, 28), load_base(5, 32)])
 
         h_q = []
         for half in range(HALVES):
-            h_rows = shared.tile([P, PACK, BANK], BF16, name="h_rows%d" % half, offset=(94 - 8 * half) * KIB)
+            h_rows = shared.tile([P, PACK, BANK], BF16, name="h_rows%d" % half, offset=(96 - 8 * half) * KIB)
             for t in range(PACK):
                 ga = gelus.tile([P, BANK], F32, name="gelu%d_%d" % (half, t), tag="gelu")
                 nc.scalar.activation(ga[:], a_acc[half, t][:], ACT.Gelu_apprx_tanh)
@@ -207,8 +208,8 @@ def tile_list_vat_crosscheck_features_kernel(
             h_woven = woven.tile([P, BANK * PACK], BF16, name="h_woven%d" % half, tag="woven", align_bytes=64)
             weave = nc.vector.tensor_copy if half == 0 else nc.scalar.copy
             weave(
-                h_woven[:].rearrange("p (c i t) -> p c t i", i=4, t=PACK),
-                h_rows[:].rearrange("p t (c i) -> p c t i", i=4),
+                h_woven[:].rearrange("p (j t) -> p j t", t=PACK),
+                h_rows[:].rearrange("p t j -> p j t"),
             )
             codes = keep.tile([P, BANK], U32, name="h_codes%d" % half, align_bytes=64)
             planes = keep.tile([P, BANK], U8, name="h_planes%d" % half, align_bytes=64)
@@ -239,43 +240,66 @@ def tile_list_vat_crosscheck_features_kernel(
         y = [keep.tile([P, PACK, PAIRS], F32, name="y%d" % g) for g in range(GROUPS)]
         buyers = {}
 
-        def pick_buyer(s):
+        def pick_buyer(s, cols):
             g, t = divmod(s, PACK)
-            u = picks.tile([P, PAIRS], F32, name="buyer%d" % s, tag="buyer")
-            nc.vector.tensor_copy(u[:], g2[s][:].indirect(second[:]))
-            nc.scalar.activation(u[:], u[:], ACT.Copy, scale=lam_sb[:, g, t : t + 1])
-            buyers[s] = u
+            if cols.start == 0:
+                buyers[s] = picks.tile([P, PAIRS], F32, name="buyer%d" % s, tag="buyer")
+            u = buyers[s][:, cols]
+            nc.vector.tensor_copy(u, g2[s][:].indirect(second[:, cols.start // 16 : cols.stop // 16]))
+            nc.scalar.activation(u, u, ACT.Copy, scale=lam_sb[:, g, t : t + 1])
 
-        def pick_seller(s):
+        def pick_seller(s, cols):
             g, t = divmod(s, PACK)
-            nc.vector.tensor_tensor(y[g][:, t, :], g2[s][:].indirect(first[:]), buyers[s][:], ALU.subtract)
-            nc.sync.dma_start(out_rows[g, t], y[g][:, t, :])
+            sellers = g2[s][:].indirect(first[:, cols.start // 16 : cols.stop // 16])
+            nc.vector.tensor_tensor(y[g][:, t, cols], sellers, buyers[s][:, cols], ALU.subtract)
+            nc.sync.dma_start(out_rows[g, t][:, cols], y[g][:, t, cols])
 
-        def planes_of(g):
-            y_woven = woven.tile([P, PAIRS * PACK], BF16, name="y_woven%d" % g, tag="woven", align_bytes=64)
-            nc.scalar.copy(
-                y_woven[:].rearrange("p (c i t) -> p c t i", i=4, t=PACK),
-                y[g][:].rearrange("p t (c i) -> p c t i", i=4),
+        y_woven = [
+            woven.tile([P, PAIRS * PACK], BF16, name="y_woven%d" % g, tag="woven", align_bytes=64) for g in range(GROUPS)
+        ]
+        y_codes = [keep.tile([P, PAIRS], U32, name="y_codes%d" % g, align_bytes=64) for g in range(GROUPS)]
+        y_planes = [keep.tile([P, PAIRS], U8, name="y_planes%d" % g, align_bytes=64) for g in range(GROUPS)]
+
+        def quantize_y(g, cols, weave):
+            packed = y_woven[g][:, PACK * cols.start : PACK * cols.stop]
+            weave(
+                packed.rearrange("p (m t) -> p m t", t=PACK),
+                y[g][:, :, cols].rearrange("p t m -> p m t"),
             )
-            codes = keep.tile([P, PAIRS], U32, name="y_codes%d" % g, align_bytes=64)
-            planes = keep.tile([P, PAIRS], U8, name="y_planes%d" % g, align_bytes=64)
-            nc.vector.quantize_mx(out=codes[:].bitcast(FP8X4), scales=planes[:], in_=y_woven[:])
-            nc.sync.dma_start(out_1[g].rearrange("p m t -> p (m t)").bitcast(I32), codes[:].bitcast(I32))
+            nc.vector.quantize_mx(out=y_codes[g][:, cols].bitcast(FP8X4), scales=y_planes[g][:, cols], in_=packed)
+            words_out = out_1[g].rearrange("p m t -> p (m t)").bitcast(I32)
+            nc.sync.dma_start(words_out[:, cols], y_codes[g][:, cols].bitcast(I32))
+
+        def store_planes(g):
             for q in range(QUADS):
-                nc.sync.dma_start(
-                    out_2[g, 4 * q : 4 * q + 4, :].bitcast(I32), planes[32 * q : 32 * q + 4, :].bitcast(I32)
+                queue = nc.scalar if q % 2 else nc.sync
+                queue.dma_start(
+                    out_2[g, 4 * q : 4 * q + 4, :].bitcast(I32), y_planes[g][32 * q : 32 * q + 4, :].bitcast(I32)
                 )
 
         slices = GROUPS * PACK
+        whole = slice(0, PAIRS)
+        front, back = slice(0, PAIRS // 2), slice(PAIRS // 2, PAIRS)
         for s in range(PACK):
             second_stage(s, 0)
-        for s in range(slices + 1):
-            if s < slices:
-                if s >= PACK:
-                    second_stage(s, 0)
-                second_stage(s, 1)
-                pick_buyer(s)
+        second_stage(0, 1)
+        for s in range(slices):
+            if s + 1 < slices:
+                if s + 1 >= PACK:
+                    second_stage(s + 1, 0)
+                second_stage(s + 1, 1)
+            if s < slices - 1:
+                pick_buyer(s, whole)
+            else:
+                pick_buyer(s, front)
+                pick_buyer(s, back)
             if s > 0:
-                pick_seller(s - 1)
-                if s % PACK == 0:
-                    planes_of(s // PACK - 1)
+                pick_seller(s - 1, whole)
+            if s == PACK:
+                quantize_y(0, whole, nc.scalar.copy)
+                store_planes(0)
+        pick_seller(slices - 1, front)
+        pick_seller(slices - 1, back)
+        quantize_y(GROUPS - 1, front, nc.scalar.copy)
+        quantize_y(GROUPS - 1, back, nc.vector.tensor_copy)
+        store_planes(GROUPS - 1)

from contextlib import ExitStack

import concourse.mybir as mybir

K, T, S, PAIRS, H, N = 1536, 4096, 1024, 512, 512, 1024
FLOPS = 2 * (2 * K * H * S + H * N * S)

F32 = mybir.dt.float32
BF16 = mybir.dt.bfloat16
I32 = mybir.dt.int32
U32 = mybir.dt.uint32
U16 = mybir.dt.uint16
U8 = mybir.dt.uint8
FP8X4 = mybir.dt.float8_e4m3fn_x4
FP4X4 = mybir.dt.float4_e2m1fn_x4
ALU = mybir.AluOpType
ACT = mybir.ActivationFunctionType

P = 128
PACK = 4
K_PASS = P * PACK
PASSES = K // K_PASS
BANK = 512
HALVES = S // BANK
GROUPS = N // K_PASS
QUADS = 4
LIVE = 100
KIB = 1024


def tile_list_vat_crosscheck_features_kernel(
    tc, tab_words, tab_scales, offs, pos1, pos2, w1, w2_words, w2_scales, gain, w3, base, lam, out_0, out_1, out_2
):
    nc = tc.nc
    with ExitStack() as ctx:
        keep = ctx.enter_context(tc.tile_pool(name="keep", bufs=1))
        shared = ctx.enter_context(tc.tile_pool(name="shared", bufs=1))
        woven = ctx.enter_context(tc.tile_pool(name="woven", bufs=4))
        gelus = ctx.enter_context(tc.tile_pool(name="gelus", bufs=5))
        picks = ctx.enter_context(tc.tile_pool(name="picks", bufs=3))
        psum = ctx.enter_context(tc.psum_pool(name="psum", bufs=1))

        def bank(i):
            return psum.tile([P, BANK], F32, name="bank%d" % i, tag="bank%d" % i)

        idx = keep.tile([P, S // 16], U16, name="idx")
        nc.sync.dma_start(idx[:], offs)
        w2_raw = shared.tile([P, PASSES, 2 * H // 4], I32, name="w2_raw", offset=38 * KIB - 1536)
        nc.sync.dma_start(w2_raw[:], w2_words.bitcast(I32).rearrange("a p c -> p a c"))
        first = keep.tile([P, PAIRS // 16], U16, name="first")
        second = keep.tile([P, PAIRS // 16], U16, name="second")

        tab_planes = shared.tile([P, T // 4], I32, name="tab_planes", offset=2 * KIB)
        w2_planes_raw = shared.tile([P, PASSES, H // 4], I32, name="w2_planes_raw", offset=0)
        moved_planes = keep.tile([P, PASSES - 1, S // 4], I32, name="moved_planes", align_bytes=64)
        nc.vector.memset(tab_planes[:], 0)
        nc.vector.memset(w2_planes_raw[:], 0)
        nc.vector.memset(moved_planes[:], 0)

        table = [shared.tile([P, T], I32, name="table%d" % a, offset=(6 + 16 * a) * KIB) for a in range(PASSES)]

        def load_table(a):
            nc.sync.dma_start(table[a][:], tab_words[a].rearrange("p t i -> p (t i)").bitcast(I32))

        nc.sync.dma_start(first[:], pos1)
        nc.sync.dma_start(second[:], pos2)
        load_table(0)
        for q in range(QUADS):
            nc.scalar.dma_start(
                tab_planes[32 * q : 32 * q + 4 * PASSES, :], tab_scales[:, 4 * q : 4 * q + 4, :].bitcast(I32)
            )
        for q in range(QUADS):
            nc.gpsimd.dma_start(
                w2_planes_raw[32 * q : 32 * q + 4, :, :],
                w2_scales[:, 4 * q : 4 * q + 4, :].bitcast(I32).rearrange("a r c -> r a c"),
            )

        w2_codes = [keep.tile([P, 2 * H], U8, name="w2_codes%d" % a, align_bytes=64) for a in range(PASSES)]
        for a in range(PASSES):
            nc.vector.tensor_copy(
                w2_codes[a][:].rearrange("p (t c m b) -> p c t m b", t=PACK, m=8, b=2),
                w2_raw[:, a, :].bitcast(U8).rearrange("p (c m t b) -> p c t m b", t=PACK, m=8, b=2),
            )
        load_table(1)
        load_table(2)

        v_planes = keep.tile([P, S], U8, name="v_planes", align_bytes=64)
        nc.vector.tensor_copy(v_planes[:], tab_planes[:].bitcast(U8).indirect(idx[:]))
        for a in range(1, PASSES):
            nc.gpsimd.dma_start(moved_planes[0:LIVE, a - 1, :], v_planes[4 * a : 4 * a + LIVE, :].bitcast(I32))

        def v_scale(a, half):
            cols = slice(half * BANK, (half + 1) * BANK)
            if a == 0:
                return v_planes[:, cols]
            return moved_planes[:, a - 1, :].bitcast(U8)[:, cols]

        w2_planes = keep.tile([P, PASSES, H], U8, name="w2_planes", align_bytes=64)
        nc.vector.tensor_copy(
            w2_planes[:].rearrange("p a (t c m) -> p a c t m", t=PACK, m=16),
            w2_planes_raw[:].bitcast(U8).rearrange("p a (c m t) -> p a c t m", t=PACK, m=16),
        )

        gain_sb = shared.tile([P, PACK], F32, name="gain_sb", offset=0)
        nc.scalar.dma_start(gain_sb[:], gain.rearrange("(p t) -> p t", t=PACK))
        lam_sb = shared.tile([P, GROUPS, PACK], F32, name="lam_sb", offset=64)
        nc.scalar.dma_start(lam_sb[:], lam.rearrange("(g p t) -> p g t", p=P, t=PACK))

        v_words = {}
        b_acc = {(half, t): bank(PACK * half + t) for half in range(HALVES) for t in range(PACK)}
        for a in range(PASSES):
            for half in range(HALVES):
                place = (1 + 2 * half) if a == 1 else (100 + 2 * a + 2 * half)
                words = shared.tile([P, BANK], U32, name="v_words%d_%d" % (a, half), offset=place * KIB, align_bytes=64)
                cols = slice(half * BANK // 16, (half + 1) * BANK // 16)
                nc.vector.tensor_copy(words[:], table[a][:].bitcast(U32).indirect(idx[:, cols]))
                v_words[a, half] = words
                for t in range(PACK):
                    nc.tensor.matmul_mx(
                        out=b_acc[half, t][:],
                        lhsT=w2_codes[a][:, 2 * P * t : 2 * P * (t + 1)].bitcast(FP4X4),
                        lhsT_scale=w2_planes[:, a, P * t : P * (t + 1)],
                        rhs=words[:].bitcast(FP8X4),
                        rhs_scale=v_scale(a, half),
                        start=(a == 0),
                        stop=(a == PASSES - 1),
                    )

        w1_raw = []
        for a, place in enumerate((4, 20, 28)):
            raw = shared.tile([P, PACK, H], F32, name="w1_raw%d" % a, offset=(2 + place) * KIB)
            nc.sync.dma_start(raw[:], w1[a * K_PASS : (a + 1) * K_PASS, :].rearrange("(p i) c -> p i c", i=PACK))
            w1_raw.append(raw)

        silu, gained_silu = {}, {}
        for half in range(HALVES):
            for t in range(PACK):
                place = 54 + 2 * (PACK * half + t)
                silu[half, t] = shared.tile([P, BANK], F32, name="silu%d_%d" % (half, t), offset=(2 + place) * KIB)
                nc.scalar.activation(silu[half, t][:], b_acc[half, t][:], ACT.Silu)

        def quantize_weight(raw, name, cast, t_runs, place):
            codes = keep.tile([P, K_PASS], U32, name=name + "_codes", align_bytes=64)
            planes = keep.tile([P, K_PASS], U8, name=name + "_planes", align_bytes=64)
            dealt = shared.tile([P, PACK * K_PASS], BF16, name=name + "_dealt", offset=(2 + place) * KIB, align_bytes=64)
            for t0, t1 in t_runs:
                cast(
                    dealt[:, K_PASS * t0 : K_PASS * t1].rearrange("p (u e m i) -> p u m e i", e=2, m=P, i=PACK),
                    raw[:].rearrange("p i (m u e) -> p u m e i", u=2, e=2)[:, t0 // 2 : t1 // 2],
                )
                nc.vector.quantize_mx(
                    out=codes[:, P * t0 : P * t1].bitcast(FP8X4),
                    scales=planes[:, P * t0 : P * t1],
                    in_=dealt[:, K_PASS * t0 : K_PASS * t1],
                )
            return codes, planes

        a_acc = {(half, t): bank(PACK * half + t) for half in range(HALVES) for t in range(PACK)}
        for a in range(PASSES):
            last = a == PASSES - 1
            codes, planes = quantize_weight(
                w1_raw[a], "w1q%d" % a, nc.vector.tensor_copy, [(0, 2), (2, 4)] if last else [(0, 4)], (36, 90, 66)[a]
            )
            if not last:
                for t in range(PACK):
                    place = 70 + 2 * (PACK * a + t)
                    sb = shared.tile([P, BANK], F32, name="gained%d_%d" % (a, t), offset=(2 + place) * KIB)
                    nc.vector.tensor_scalar(sb[:], silu[a, t][:], gain_sb[:, t : t + 1], None, ALU.mult)
                    gained_silu[a, t] = sb
            for half in range(HALVES):
                for t in range(PACK):
                    nc.tensor.matmul_mx(
                        out=a_acc[half, t][:],
                        lhsT=codes[:, P * t : P * (t + 1)].bitcast(FP8X4),
                        lhsT_scale=planes[:, P * t : P * (t + 1)],
                        rhs=v_words[a, half][:].bitcast(FP8X4),
                        rhs_scale=v_scale(a, half),
                        start=(a == 0),
                        stop=last,
                    )

        base_rows = base.rearrange("(g p t) j -> g t p j", p=P, t=PACK)

        def load_w3(g, place):
            raw = shared.tile([P, PACK, K_PASS], F32, name="w3_raw%d" % g, offset=(2 + place) * KIB)
            nc.sync.dma_start(raw[:], w3[:, g * K_PASS : (g + 1) * K_PASS].rearrange("(p i) c -> p i c", i=PACK))
            return raw

        def load_base(s, place):
            rows = shared.tile([P, S], F32, name="g2_%d" % s, offset=(2 + place) * KIB)
            nc.sync.dma_start(rows[:], base_rows[s // PACK, s % PACK])
            return rows

        w3_raw = [load_w3(0, 40)]
        g2 = [load_base(s, place) for s, place in enumerate((48, 4, 8, 36))]
        w3_raw.append(load_w3(1, 20))
        g2.extend([load_base(4, 28), load_base(5, 32)])

        h_q = []
        for half in range(HALVES):
            h_rows = shared.tile([P, PACK, BANK], BF16, name="h_rows%d" % half, offset=(96 - 8 * half) * KIB)
            for t in range(PACK):
                ga = gelus.tile([P, BANK], F32, name="gelu%d_%d" % (half, t), tag="gelu")
                nc.scalar.activation(ga[:], a_acc[half, t][:], ACT.Gelu_apprx_tanh)
                nc.vector.scalar_tensor_tensor(
                    h_rows[:, t, :], ga[:], gain_sb[:, t : t + 1], gained_silu[half, t][:], ALU.mult, ALU.subtract
                )
            h_woven = woven.tile([P, BANK * PACK], BF16, name="h_woven%d" % half, tag="woven", align_bytes=64)
            weave = nc.vector.tensor_copy if half == 0 else nc.scalar.copy
            weave(
                h_woven[:].rearrange("p (j t) -> p j t", t=PACK),
                h_rows[:].rearrange("p t j -> p j t"),
            )
            codes = keep.tile([P, BANK], U32, name="h_codes%d" % half, align_bytes=64)
            planes = keep.tile([P, BANK], U8, name="h_planes%d" % half, align_bytes=64)
            nc.vector.quantize_mx(out=codes[:].bitcast(FP8X4), scales=planes[:], in_=h_woven[:])
            h_q.append((codes, planes))
            if half == 0:
                w3_q = [quantize_weight(w3_raw[0], "w3q0", nc.scalar.copy, [(0, 2), (2, 4)], 74)]
        g2.extend([load_base(6, 40), load_base(7, 44)])
        w3_q.append(quantize_weight(w3_raw[1], "w3q1", nc.scalar.copy, [(0, 4)], 86))

        def second_stage(s, half):
            g, t = divmod(s, PACK)
            acc = bank(PACK * half + t)
            codes, planes = w3_q[g]
            nc.tensor.matmul_mx(
                out=acc[:],
                lhsT=codes[:, P * t : P * (t + 1)].bitcast(FP8X4),
                lhsT_scale=planes[:, P * t : P * (t + 1)],
                rhs=h_q[half][0][:].bitcast(FP8X4),
                rhs_scale=h_q[half][1][:],
                start=True,
                stop=True,
            )
            cols = slice(half * BANK, (half + 1) * BANK)
            nc.vector.tensor_tensor(g2[s][:, cols], acc[:], g2[s][:, cols], ALU.max)

        out_rows = out_0.rearrange("(g p t) m -> g t p m", p=P, t=PACK)
        y = [keep.tile([P, PACK, PAIRS], F32, name="y%d" % g) for g in range(GROUPS)]
        buyers = {}

        def pick_buyer(s, cols):
            g, t = divmod(s, PACK)
            if cols.start == 0:
                buyers[s] = picks.tile([P, PAIRS], F32, name="buyer%d" % s, tag="buyer")
            u = buyers[s][:, cols]
            nc.vector.tensor_copy(u, g2[s][:].indirect(second[:, cols.start // 16 : cols.stop // 16]))
            nc.scalar.activation(u, u, ACT.Copy, scale=lam_sb[:, g, t : t + 1])

        def pick_seller(s, cols):
            g, t = divmod(s, PACK)
            sellers = g2[s][:].indirect(first[:, cols.start // 16 : cols.stop // 16])
            nc.vector.tensor_tensor(y[g][:, t, cols], sellers, buyers[s][:, cols], ALU.subtract)
            nc.sync.dma_start(out_rows[g, t][:, cols], y[g][:, t, cols])

        y_woven = [
            woven.tile([P, PAIRS * PACK], BF16, name="y_woven%d" % g, tag="woven", align_bytes=64) for g in range(GROUPS)
        ]
        y_codes = [keep.tile([P, PAIRS], U32, name="y_codes%d" % g, align_bytes=64) for g in range(GROUPS)]
        y_planes = [keep.tile([P, PAIRS], U8, name="y_planes%d" % g, align_bytes=64) for g in range(GROUPS)]

        def quantize_y(g, cols, weave):
            packed = y_woven[g][:, PACK * cols.start : PACK * cols.stop]
            weave(
                packed.rearrange("p (m t) -> p m t", t=PACK),
                y[g][:, :, cols].rearrange("p t m -> p m t"),
            )
            nc.vector.quantize_mx(out=y_codes[g][:, cols].bitcast(FP8X4), scales=y_planes[g][:, cols], in_=packed)
            words_out = out_1[g].rearrange("p m t -> p (m t)").bitcast(I32)
            nc.sync.dma_start(words_out[:, cols], y_codes[g][:, cols].bitcast(I32))

        def store_planes(g):
            for q in range(QUADS):
                queue = nc.scalar if q % 2 else nc.sync
                queue.dma_start(
                    out_2[g, 4 * q : 4 * q + 4, :].bitcast(I32), y_planes[g][32 * q : 32 * q + 4, :].bitcast(I32)
                )

        slices = GROUPS * PACK
        whole = slice(0, PAIRS)
        front, back = slice(0, PAIRS // 2), slice(PAIRS // 2, PAIRS)
        for s in range(PACK):
            second_stage(s, 0)
        second_stage(0, 1)
        for s in range(slices):
            if s + 1 < slices:
                if s + 1 >= PACK:
                    second_stage(s + 1, 0)
                second_stage(s + 1, 1)
            if s < slices - 1:
                pick_buyer(s, whole)
            else:
                pick_buyer(s, front)
                pick_buyer(s, back)
            if s > 0:
                pick_seller(s - 1, whole)
            if s == PACK:
                quantize_y(0, whole, nc.scalar.copy)
                store_planes(0)
        pick_seller(slices - 1, front)
        pick_seller(slices - 1, back)
        quantize_y(GROUPS - 1, front, nc.scalar.copy)
        quantize_y(GROUPS - 1, back, nc.vector.tensor_copy)
        store_planes(GROUPS - 1)
